import numpy as np
import ml_dtypes


def mxq(x, axis, fmt="e4m3"):
    dtype, down = {"e4m3": (ml_dtypes.float8_e4m3fn, 7), "e5m2": (ml_dtypes.float8_e5m2, 14)}[fmt]
    v = np.moveaxis(np.asarray(x, np.float32).astype(ml_dtypes.bfloat16).astype(np.float64), axis, -1)
    blocks = v.reshape(v.shape[:-1] + (-1, 32))
    amax = np.abs(blocks).max(-1, keepdims=True)
    byte = np.maximum(np.where(amax > 0, np.frexp(amax)[1] - 1 + 127, 0) - down, 1)
    scale = np.exp2(byte - 127.0)
    codes = (blocks / scale).astype(np.float32).astype(dtype).astype(np.float64)
    return np.moveaxis((codes * scale).reshape(v.shape), -1, axis)


WIDE = False


def mx_kscale(k):
    if not WIDE:
        return np.ones(k)
    levels = np.array([10, -10, 5, -5, 0])
    if k % 512:
        return np.exp2(np.random.permutation(np.resize(levels, k // 32))).repeat(32)
    a = np.empty((k // 512, 16))
    for p in range(k // 512):
        a[p, :8] = np.random.permutation(np.resize(levels, 8))
        for g in range(8):
            far = levels[np.abs(levels - a[p, g]) >= 10]
            a[p, g + 8] = far[np.random.randint(len(far))]
    return np.exp2(a.ravel()).repeat(32)


def f64(x):
    return np.asarray(x).astype(np.float64)


def striped(idx):
    return np.tile(idx.reshape(-1, 16).T, (8, 1)).astype(np.uint16)


def unstriped(offs):
    return offs[:16].T.reshape(-1).astype(np.int64)


def striped8(idx):
    return np.concatenate([x.reshape(-1, 16).T for x in idx]).astype(np.uint16)


def runs(offs, k):
    lists = np.stack([offs[16 * r : 16 * r + 16].T.reshape(-1) for r in range(8)]).astype(np.int64)
    return lists[np.arange(k) % 512 // 64]


def pack_weight(w):
    k, n = w.shape
    w = f64(np.asarray(w, np.float32).astype(ml_dtypes.bfloat16)).reshape(k // 32, 32, n)
    amax = np.abs(w).max(1)
    byte = np.clip(np.where(amax > 0, np.frexp(amax)[1] - 1 + 127 - 7, 1), 1, 254)
    scaled = (w * np.exp2(127.0 - byte)[:, None, :]).reshape(k, n).astype(np.float32)
    words = np.ascontiguousarray(scaled.reshape(k // 512, 128, 4, n).transpose(0, 1, 3, 2)).astype(ml_dtypes.float8_e4m3fn).view(np.uint8)
    return words, np.ascontiguousarray(byte.astype(np.uint8).reshape(k // 512, 16, n))


def unpack_weight(words, scales):
    g, p, n, _ = words.shape
    vals = np.ascontiguousarray(words).view(ml_dtypes.float8_e4m3fn).astype(np.float64) * np.repeat(np.exp2(scales.astype(np.float64) - 127.0), 8, axis=1)[..., None]
    return vals.transpose(0, 1, 3, 2).reshape(g * 512, n)

def planes(y):
    n, m = y.shape
    v = y.astype(np.float32).astype(ml_dtypes.bfloat16).astype(np.float64).reshape(n // 32, 32, m)
    top = np.abs(v).max(1)
    byte = np.clip(np.where(top > 0, np.frexp(top)[1] - 1 + 127 - 7, 1), 1, 254)
    codes = (v * np.exp2(127.0 - byte)[:, None, :]).reshape(n, m).astype(np.float32).astype(ml_dtypes.float8_e4m3fn).view(np.uint8)
    words = codes.reshape(n // 512, 128, 4, m).transpose(0, 1, 3, 2)
    return np.ascontiguousarray(words), np.ascontiguousarray(byte.astype(np.uint8).reshape(n // 512, 16, m))


K, T, S, N, H = 512, 2048, 512, 512, 512


def setup_inputs():
    n = np.random.standard_normal
    s = mx_kscale(K)[:, None]
    u = mx_kscale(H)
    packed_xT = pack_weight(n((K, T)) * s)
    packed_w1 = pack_weight(n((K, H)) / np.sqrt(K) / s)
    packed_w2 = pack_weight(n((H, N)) / np.sqrt(H) / u[:, None])
    return {
        "x_words": packed_xT[0],
        "x_scales": packed_xT[1],
        "w1_words": packed_w1[0],
        "w1_scales": packed_w1[1],
        "gn": (np.random.uniform(0.5, 1.5, (H, 1)) * u[:, None]).astype(np.float32),
        "w2_words": packed_w2[0],
        "w2_scales": packed_w2[1],
        "res": (2 * n((N, S))).astype(np.float32),
        "offs": striped(np.random.permutation(T)[:S]),
        "o1": striped8(np.stack([np.random.permutation(S) for _ in range(8)])),
        "o2": striped8(np.stack([np.random.permutation(S) for _ in range(8)])),
        "i1": striped8(np.stack([np.random.permutation(S) for _ in range(8)])),
        "i2": striped8(np.stack([np.random.permutation(S) for _ in range(8)])),
    }


def reference(x_words, x_scales, w1_words, w1_scales, gn, w2_words, w2_scales, res, offs, o1, o2, i1, i2):
    xq = unpack_weight(x_words, x_scales)[:, unstriped(offs)]
    y = unpack_weight(w1_words, w1_scales).T @ xq
    hub = y[np.arange(H)[:, None], runs(o1, H)] + y[np.arange(H)[:, None], runs(o2, H)]
    hn = hub / (np.sqrt((hub) ** 2 + 1))
    z = f64(gn) * (hn[np.arange(H)[:, None], runs(i1, H)] + hn[np.arange(H)[:, None], runs(i2, H)])
    out_0 = f64(res) + (unpack_weight(w2_words, w2_scales).T @ mxq(z, 0, "e4m3"))
    return (out_0,) + planes(out_0)

@@ -1,0 +1,215 @@
+from contextlib import ExitStack
+
+import concourse.mybir as mybir
+
+F32 = mybir.dt.float32
+BF16 = mybir.dt.bfloat16
+I32 = mybir.dt.int32
+U32 = mybir.dt.uint32
+U16 = mybir.dt.uint16
+U8 = mybir.dt.uint8
+FP8X4 = mybir.dt.float8_e4m3fn_x4
+ACT = mybir.ActivationFunctionType
+ALU = mybir.AluOpType
+
+P = 128
+PACK = 4
+T = 2048
+S = 512
+H = 512
+HALF = 256
+CHUNKS = ((0, 256), (256, 128), (384, 128))
+FLOPS = 2 * 2 * 512 * 512 * 512
+
+
+def tile_picked_hubauth_none_po_kernel(
+    tc, x_words, x_scales, w1_words, w1_scales, gn, w2_words, w2_scales, res, offs, o1, o2, i1, i2,
+    out_0, out_1, out_2,
+):
+    nc = tc.nc
+    with ExitStack() as ctx:
+        lists = ctx.enter_context(tc.tile_pool(name="lists", bufs=1))
+        keep = ctx.enter_context(tc.tile_pool(name="keep", bufs=1))
+        psum = ctx.enter_context(tc.psum_pool(name="psum", bufs=1))
+
+        def words_view(dram):
+            return dram[0].rearrange("p n t -> p (n t)").bitcast(I32)
+
+        def load_scale_rows(engines, plane, dram):
+            for q, engine in enumerate(engines):
+                engine.dma_start(out=plane[32 * q : 32 * q + 4, :].bitcast(I32), in_=dram[0, 4 * q : 4 * q + 4, :].bitcast(I32))
+
+        def load_list(dram, name):
+            tile = lists.tile([P, S // 16], U16, name=name)
+            nc.sync.dma_start(tile[:], dram)
+            return tile
+
+        def cols(tile, start, n):
+            return tile[:, start // 16 : (start + n) // 16]
+
+        x_s = keep.tile([P, T], U8, name="x_s", tag="g0", align_bytes=64)
+        w_s_raw = keep.tile([P, H], U8, name="w_s_raw", align_bytes=64)
+        nc.gpsimd.memset(x_s[:].bitcast(I32), 0)
+        nc.vector.memset(w_s_raw[:].bitcast(I32), 0)
+
+        offs_t = load_list(offs, "offs_t")
+        gain = keep.tile([P, PACK], F32, name="gain")
+        nc.scalar.dma_start(out=gain[:], in_=gn.rearrange("(p t) o -> p (t o)", t=PACK))
+        x_w = keep.tile([P, T], U32, name="x_w", tag="big", align_bytes=64)
+        nc.scalar.dma_start(out=x_w[:].bitcast(I32), in_=words_view(x_words))
+        w1_raw = keep.tile([P, H], U32, name="w1_raw", tag="w_raw", align_bytes=64)
+        nc.scalar.dma_start(out=w1_raw[:].bitcast(I32), in_=words_view(w1_words))
+        load_scale_rows([nc.sync] * 4, x_s, x_scales)
+        load_scale_rows([nc.gpsimd, nc.gpsimd, nc.sync, nc.sync], w_s_raw, w1_scales)
+        o1_t = load_list(o1, "o1_t")
+        o2_t = load_list(o2, "o2_t")
+        i1_t = load_list(i1, "i1_t")
+        i2_t = load_list(i2, "i2_t")
+
+        def deal(copy, dealt, raw):
+            copy(out=dealt[:].rearrange("p (t m) -> p m t", t=PACK), in_=raw[:].rearrange("p (m t) -> p m t", t=PACK))
+
+        warm = keep.tile([P, 1], F32, name="warm")
+        nc.scalar.activation(warm[:], gain[:, 0:1], ACT.Abs_reciprocal_sqrt, bias=1.0)
+        w1_w = keep.tile([P, H], U32, name="w1_w", align_bytes=64)
+        w1_s = keep.tile([P, H], U8, name="w1_s", align_bytes=64)
+        deal(nc.scalar.copy, w1_w, w1_raw)
+
+        g_s = keep.tile([P, S], U8, name="g_s", align_bytes=64)
+        nc.vector.tensor_copy(g_s[:], x_s[:].indirect(offs_t[:]))
+        deal(nc.vector.tensor_copy, w1_s, w_s_raw)
+
+        y = [keep.tile([P, S], F32, name="y%d" % t) for t in range(PACK)]
+        y_ps = {}
+        for h in range(2):
+            g_w = keep.tile([P, HALF], U32, name="g_w%d" % h, tag="g%d" % h, align_bytes=64)
+            nc.vector.tensor_copy(g_w[:], x_w[:].indirect(cols(offs_t, h * HALF, HALF)))
+            for t in range(PACK):
+                acc = psum.tile([P, HALF], F32, name="y_ps", tag="bank%d" % (4 * h + t))
+                nc.tensor.matmul_mx(
+                    out=acc[:],
+                    lhsT=w1_w[:, t * P : (t + 1) * P].bitcast(FP8X4),
+                    lhsT_scale=w1_s[:, t * P : (t + 1) * P],
+                    rhs=g_w[:].bitcast(FP8X4),
+                    rhs_scale=g_s[:, h * HALF : (h + 1) * HALF],
+                    start=True,
+                    stop=True,
+                )
+                y_ps[h, t] = acc
+
+        w2_raw = keep.tile([P, H], U32, name="w2_raw", tag="w_raw", align_bytes=64)
+        nc.sync.dma_start(out=w2_raw[:].bitcast(I32), in_=words_view(w2_words))
+        load_scale_rows([nc.sync] * 4, w_s_raw, w2_scales)
+        res_t = keep.tile([P, PACK, S], F32, name="res_t", tag="big", align_bytes=64)
+        nc.sync.dma_start(out=res_t[:], in_=res.rearrange("(p t) j -> p t j", t=PACK))
+        w2_w = keep.tile([P, H], U32, name="w2_w", align_bytes=64)
+        w2_s = keep.tile([P, H], U8, name="w2_s", align_bytes=64)
+
+        hub = [keep.tile([P, S], F32, name="hub%d" % t) for t in range(PACK)]
+        hn = [keep.tile([P, S], F32, name="hn%d" % t) for t in range(PACK)]
+
+        def evacuate(t):
+            nc.scalar.copy(out=y[t][:, 0:HALF], in_=y_ps[0, t][:])
+            nc.vector.tensor_copy(out=y[t][:, HALF:S], in_=y_ps[1, t][:])
+
+        def hubs(t):
+            for h in range(2):
+                first = keep.tile([P, HALF], F32, name="first%d_%d" % (t, h))
+                nc.scalar.activation(first[:], y[t][:].indirect(cols(o1_t, h * HALF, HALF)), ACT.Copy)
+                nc.vector.tensor_tensor(
+                    hub[t][:, h * HALF : (h + 1) * HALF], y[t][:].indirect(cols(o2_t, h * HALF, HALF)), first[:], ALU.add
+                )
+
+        def normalise(t):
+            square = keep.tile([P, S], F32, name="square%d" % t)
+            root = keep.tile([P, S], F32, name="root%d" % t)
+            if t == PACK - 1:
+                nc.vector.tensor_tensor(square[:], hub[t][:], hub[t][:], ALU.mult)
+            else:
+                nc.scalar.activation(square[:], hub[t][:], ACT.Square)
+            nc.scalar.activation(root[:], square[:], ACT.Abs_reciprocal_sqrt, bias=1.0)
+            nc.vector.scalar_tensor_tensor(hn[t][:], hub[t][:], gain[:, t : t + 1], root[:], ALU.mult, ALU.mult)
+
+        z = [keep.tile([P, PACK, n], F32, name="z%d" % c) for c, (j0, n) in enumerate(CHUNKS)]
+
+        def authorities(t, c):
+            j0, n = CHUNKS[c]
+            one = keep.tile([P, n], F32, name="one%d_%d" % (t, c))
+            nc.scalar.activation(one[:], hn[t][:].indirect(cols(i1_t, j0, n)), ACT.Copy)
+            nc.vector.tensor_tensor(z[c][:, t, :], hn[t][:].indirect(cols(i2_t, j0, n)), one[:], ALU.add)
+
+        def interleave(copy, grouped, planes):
+            copy(
+                out=grouped[:].rearrange("p (c i) t -> p c t i", i=4),
+                in_=planes[:].rearrange("p t (c i) -> p c t i", i=4),
+            )
+
+        out_s = keep.tile([P, S], U8, name="out_s", align_bytes=64)
+        out_rows = out_0.rearrange("(p t) j -> p t j", t=PACK)
+        out_words = words_view(out_1)
+
+        def second_product(c):
+            j0, n = CHUNKS[c]
+            z_b = keep.tile([P, n, PACK], BF16, name="z_b%d" % c, align_bytes=64)
+            interleave(nc.vector.tensor_copy if c == len(CHUNKS) - 1 else nc.scalar.copy, z_b, z[c])
+            z_w = keep.tile([P, n], U32, name="z_w%d" % c, align_bytes=64)
+            z_s = keep.tile([P, n], U8, name="z_s%d" % c, align_bytes=64)
+            nc.vector.quantize_mx(out=z_w[:].bitcast(FP8X4), scales=z_s[:], in_=z_b[:].rearrange("p j t -> p (j t)"))
+            per_bank = S // n
+            banks = []
+            for b in range(PACK // per_bank):
+                acc = psum.tile([P, per_bank, n], F32, name="o_ps", tag="bank%d" % (j0 // P + b))
+                for u in range(per_bank):
+                    t = b * per_bank + u
+                    nc.tensor.matmul_mx(
+                        out=acc[:, u, :],
+                        lhsT=w2_w[:, t * P : (t + 1) * P].bitcast(FP8X4),
+                        lhsT_scale=w2_s[:, t * P : (t + 1) * P],
+                        rhs=z_w[:].bitcast(FP8X4),
+                        rhs_scale=z_s[:],
+                        start=True,
+                        stop=True,
+                    )
+                banks.append(acc)
+            return banks
+
+        def hand_out(c, banks):
+            j0, n = CHUNKS[c]
+            per_bank = S // n
+            result = keep.tile([P, PACK, n], F32, name="result%d" % c)
+            for b, acc in enumerate(banks):
+                rows = slice(b * per_bank, (b + 1) * per_bank)
+                nc.vector.tensor_tensor(result[:, rows, :], acc[:], res_t[:, rows, j0 : j0 + n], ALU.add)
+            nc.sync.dma_start(out=out_rows[:, :, j0 : j0 + n], in_=result[:])
+            r_b = keep.tile([P, n, PACK], BF16, name="r_b%d" % c, align_bytes=64)
+            interleave(nc.vector.tensor_copy if c == len(CHUNKS) - 1 else nc.scalar.copy, r_b, result)
+            r_w = keep.tile([P, n], U32, name="r_w%d" % c, align_bytes=64)
+            nc.vector.quantize_mx(
+                out=r_w[:].bitcast(FP8X4), scales=out_s[:, j0 : j0 + n], in_=r_b[:].rearrange("p j t -> p (j t)")
+            )
+            nc.sync.dma_start(out=out_words[:, j0 : j0 + n], in_=r_w[:].bitcast(I32))
+
+        evacuate(0)
+        evacuate(1)
+        hubs(0)
+        for t in range(1, PACK):
+            if t + 1 < PACK:
+                evacuate(t + 1)
+            hubs(t)
+            normalise(t - 1)
+            if t == 2:
+                deal(nc.vector.tensor_copy, w2_s, w_s_raw)
+                deal(nc.scalar.copy, w2_w, w2_raw)
+        normalise(PACK - 1)
+        for t in range(PACK):
+            authorities(t, 0)
+        banks = second_product(0)
+        for c in range(1, len(CHUNKS)):
+            for t in range(PACK):
+                authorities(t, c)
+            following = second_product(c)
+            hand_out(c - 1, banks)
+            banks = following
+        hand_out(len(CHUNKS) - 1, banks)
+        for q in range(4):
+            nc.scalar.dma_start(out=out_2[0, 4 * q : 4 * q + 4, :].bitcast(I32), in_=out_s[32 * q : 32 * q + 4, :].bitcast(I32))

@@ -18,7 +18,8 @@ T = 2048
 S = 512
 H = 512
 HALF = 256
-CHUNKS = ((0, 256), (256, 128), (384, 128))
+CHUNKS = ((0, 128), (128, 128), (256, 128), (384, 128))
+GATHERS = ((0, 256), (256, 256))
 FLOPS = 2 * 2 * 512 * 512 * 512
 
 
@@ -66,31 +67,43 @@ def tile_picked_hubauth_none_po_kernel(
         i1_t = load_list(i1, "i1_t")
         i2_t = load_list(i2, "i2_t")
 
-        def deal(copy, dealt, raw):
-            copy(out=dealt[:].rearrange("p (t m) -> p m t", t=PACK), in_=raw[:].rearrange("p (m t) -> p m t", t=PACK))
+        def deal_words(dealt, raw):
+            nc.scalar.copy(
+                out=dealt[:].rearrange("p (t c i) -> p c t i", t=PACK, i=4),
+                in_=raw[:].rearrange("p (c i t) -> p c t i", t=PACK, i=4),
+            )
+
+        def deal_scales(dealt, raw):
+            nc.vector.tensor_copy(
+                out=dealt[:].rearrange("p (t m) -> p t m", t=PACK), in_=raw[:].rearrange("p (m t) -> p t m", t=PACK)
+            )
 
         warm = keep.tile([P, 1], F32, name="warm")
         nc.scalar.activation(warm[:], gain[:, 0:1], ACT.Abs_reciprocal_sqrt, bias=1.0)
         w1_w = keep.tile([P, H], U32, name="w1_w", align_bytes=64)
         w1_s = keep.tile([P, H], U8, name="w1_s", align_bytes=64)
-        deal(nc.scalar.copy, w1_w, w1_raw)
+        deal_words(w1_w, w1_raw)
 
         g_s = keep.tile([P, S], U8, name="g_s", align_bytes=64)
         nc.vector.tensor_copy(g_s[:], x_s[:].indirect(offs_t[:]))
-        deal(nc.vector.tensor_copy, w1_s, w_s_raw)
+        g_w = []
+        for h in range(2):
+            half = keep.tile([P, HALF], U32, name="g_w%d" % h, tag="g%d" % h, align_bytes=64)
+            nc.vector.tensor_copy(half[:], x_w[:].indirect(cols(offs_t, h * HALF, HALF)))
+            g_w.append(half)
+            if h == 0:
+                deal_scales(w1_s, w_s_raw)
 
         y = [keep.tile([P, S], F32, name="y%d" % t) for t in range(PACK)]
         y_ps = {}
-        for h in range(2):
-            g_w = keep.tile([P, HALF], U32, name="g_w%d" % h, tag="g%d" % h, align_bytes=64)
-            nc.vector.tensor_copy(g_w[:], x_w[:].indirect(cols(offs_t, h * HALF, HALF)))
-            for t in range(PACK):
+        for t in range(PACK):
+            for h in range(2):
                 acc = psum.tile([P, HALF], F32, name="y_ps", tag="bank%d" % (4 * h + t))
                 nc.tensor.matmul_mx(
                     out=acc[:],
                     lhsT=w1_w[:, t * P : (t + 1) * P].bitcast(FP8X4),
                     lhsT_scale=w1_s[:, t * P : (t + 1) * P],
-                    rhs=g_w[:].bitcast(FP8X4),
+                    rhs=g_w[h][:].bitcast(FP8X4),
                     rhs_scale=g_s[:, h * HALF : (h + 1) * HALF],
                     start=True,
                     stop=True,
@@ -112,51 +125,55 @@ def tile_picked_hubauth_none_po_kernel(
             nc.scalar.copy(out=y[t][:, 0:HALF], in_=y_ps[0, t][:])
             nc.vector.tensor_copy(out=y[t][:, HALF:S], in_=y_ps[1, t][:])
 
-        def hubs(t):
-            for h in range(2):
-                first = keep.tile([P, HALF], F32, name="first%d_%d" % (t, h))
-                nc.scalar.activation(first[:], y[t][:].indirect(cols(o1_t, h * HALF, HALF)), ACT.Copy)
-                nc.vector.tensor_tensor(
-                    hub[t][:, h * HALF : (h + 1) * HALF], y[t][:].indirect(cols(o2_t, h * HALF, HALF)), first[:], ALU.add
-                )
+        def hubs(t, h):
+            first = keep.tile([P, HALF], F32, name="first%d_%d" % (t, h))
+            nc.scalar.activation(first[:], y[t][:].indirect(cols(o1_t, h * HALF, HALF)), ACT.Copy)
+            nc.vector.tensor_tensor(
+                hub[t][:, h * HALF : (h + 1) * HALF], y[t][:].indirect(cols(o2_t, h * HALF, HALF)), first[:], ALU.add
+            )
+
+        square = [keep.tile([P, S], F32, name="square%d" % t) for t in range(PACK)]
+
+        def squares(t):
+            if "SSSV"[t] == "V":
+                nc.vector.tensor_tensor(square[t][:], hub[t][:], hub[t][:], ALU.mult)
+            else:
+                nc.scalar.activation(square[t][:], hub[t][:], ACT.Square)
 
         def normalise(t):
-            square = keep.tile([P, S], F32, name="square%d" % t)
             root = keep.tile([P, S], F32, name="root%d" % t)
-            if t == PACK - 1:
-                nc.vector.tensor_tensor(square[:], hub[t][:], hub[t][:], ALU.mult)
-            else:
-                nc.scalar.activation(square[:], hub[t][:], ACT.Square)
-            nc.scalar.activation(root[:], square[:], ACT.Abs_reciprocal_sqrt, bias=1.0)
+            nc.scalar.activation(root[:], square[t][:], ACT.Abs_reciprocal_sqrt, bias=1.0)
             nc.vector.scalar_tensor_tensor(hn[t][:], hub[t][:], gain[:, t : t + 1], root[:], ALU.mult, ALU.mult)
 
-        z = [keep.tile([P, PACK, n], F32, name="z%d" % c) for c, (j0, n) in enumerate(CHUNKS)]
+        z = keep.tile([P, PACK, S], F32, name="z")
 
-        def authorities(t, c):
-            j0, n = CHUNKS[c]
-            one = keep.tile([P, n], F32, name="one%d_%d" % (t, c))
+        def authorities(t, j0, n):
+            one = keep.tile([P, n], F32, name="one%d_%d" % (t, j0))
             nc.scalar.activation(one[:], hn[t][:].indirect(cols(i1_t, j0, n)), ACT.Copy)
-            nc.vector.tensor_tensor(z[c][:, t, :], hn[t][:].indirect(cols(i2_t, j0, n)), one[:], ALU.add)
+            nc.vector.tensor_tensor(z[:, t, j0 : j0 + n], hn[t][:].indirect(cols(i2_t, j0, n)), one[:], ALU.add)
 
-        def interleave(copy, grouped, planes):
-            copy(
-                out=grouped[:].rearrange("p (c i) t -> p c t i", i=4),
-                in_=planes[:].rearrange("p t (c i) -> p c t i", i=4),
-            )
+        def interleave(engine, grouped, planes):
+            copy = nc.vector.tensor_copy if engine == "V" else nc.scalar.copy
+            copy(out=grouped[:], in_=planes.rearrange("p t j -> p j t"))
 
         out_s = keep.tile([P, S], U8, name="out_s", align_bytes=64)
         out_rows = out_0.rearrange("(p t) j -> p t j", t=PACK)
         out_words = words_view(out_1)
 
+        z_b, banks, result, r_b = {}, {}, {}, {}
+
+        def round_z(c):
+            j0, n = CHUNKS[c]
+            z_b[c] = keep.tile([P, n, PACK], BF16, name="z_b%d" % c, align_bytes=64)
+            interleave("SSSV"[c], z_b[c], z[:, :, j0 : j0 + n])
+
         def second_product(c):
             j0, n = CHUNKS[c]
-            z_b = keep.tile([P, n, PACK], BF16, name="z_b%d" % c, align_bytes=64)
-            interleave(nc.vector.tensor_copy if c == len(CHUNKS) - 1 else nc.scalar.copy, z_b, z[c])
             z_w = keep.tile([P, n], U32, name="z_w%d" % c, align_bytes=64)
             z_s = keep.tile([P, n], U8, name="z_s%d" % c, align_bytes=64)
-            nc.vector.quantize_mx(out=z_w[:].bitcast(FP8X4), scales=z_s[:], in_=z_b[:].rearrange("p j t -> p (j t)"))
+            nc.vector.quantize_mx(out=z_w[:].bitcast(FP8X4), scales=z_s[:], in_=z_b[c][:].rearrange("p j t -> p (j t)"))
             per_bank = S // n
-            banks = []
+            banks[c] = []
             for b in range(PACK // per_bank):
                 acc = psum.tile([P, per_bank, n], F32, name="o_ps", tag="bank%d" % (j0 // P + b))
                 for u in range(per_bank):
@@ -170,46 +187,62 @@ def tile_picked_hubauth_none_po_kernel(
                         start=True,
                         stop=True,
                     )
-                banks.append(acc)
-            return banks
+                banks[c].append(acc)
 
-        def hand_out(c, banks):
+        def add_residual(c):
             j0, n = CHUNKS[c]
             per_bank = S // n
-            result = keep.tile([P, PACK, n], F32, name="result%d" % c)
-            for b, acc in enumerate(banks):
+            result[c] = keep.tile([P, PACK, n], F32, name="result%d" % c)
+            for b, acc in enumerate(banks[c]):
                 rows = slice(b * per_bank, (b + 1) * per_bank)
-                nc.vector.tensor_tensor(result[:, rows, :], acc[:], res_t[:, rows, j0 : j0 + n], ALU.add)
-            nc.sync.dma_start(out=out_rows[:, :, j0 : j0 + n], in_=result[:])
-            r_b = keep.tile([P, n, PACK], BF16, name="r_b%d" % c, align_bytes=64)
-            interleave(nc.vector.tensor_copy if c == len(CHUNKS) - 1 else nc.scalar.copy, r_b, result)
+                nc.vector.tensor_tensor(result[c][:, rows, :], acc[:], res_t[:, rows, j0 : j0 + n], ALU.add)
+            nc.sync.dma_start(out=out_rows[:, :, j0 : j0 + n], in_=result[c][:])
+
+        def round_result(c):
+            j0, n = CHUNKS[c]
+            r_b[c] = keep.tile([P, n, PACK], BF16, name="r_b%d" % c, align_bytes=64)
+            interleave("SSSV"[c], r_b[c], result[c][:])
+
+        def hand_out(c):
+            j0, n = CHUNKS[c]
             r_w = keep.tile([P, n], U32, name="r_w%d" % c, align_bytes=64)
             nc.vector.quantize_mx(
-                out=r_w[:].bitcast(FP8X4), scales=out_s[:, j0 : j0 + n], in_=r_b[:].rearrange("p j t -> p (j t)")
+                out=r_w[:].bitcast(FP8X4), scales=out_s[:, j0 : j0 + n], in_=r_b[c][:].rearrange("p j t -> p (j t)")
             )
             nc.sync.dma_start(out=out_words[:, j0 : j0 + n], in_=r_w[:].bitcast(I32))
 
         evacuate(0)
         evacuate(1)
-        hubs(0)
-        for t in range(1, PACK):
-            if t + 1 < PACK:
-                evacuate(t + 1)
-            hubs(t)
-            normalise(t - 1)
-            if t == 2:
-                deal(nc.vector.tensor_copy, w2_s, w_s_raw)
-                deal(nc.scalar.copy, w2_w, w2_raw)
-        normalise(PACK - 1)
         for t in range(PACK):
-            authorities(t, 0)
-        banks = second_product(0)
-        for c in range(1, len(CHUNKS)):
-            for t in range(PACK):
-                authorities(t, c)
-            following = second_product(c)
-            hand_out(c - 1, banks)
-            banks = following
-        hand_out(len(CHUNKS) - 1, banks)
+            if 0 < t < PACK - 1:
+                evacuate(t + 1)
+            hubs(t, 0)
+            if t > 1:
+                normalise(t - 2)
+            hubs(t, 1)
+            if t > 0:
+                squares(t - 1)
+        normalise(PACK - 2)
+        squares(PACK - 1)
+        normalise(PACK - 1)
+        deal_scales(w2_s, w_s_raw)
+        deal_words(w2_w, w2_raw)
+        for c in range(len(CHUNKS) + 1):
+            inside = c < len(CHUNKS)
+            if inside:
+                for j0, n in GATHERS:
+                    if j0 == CHUNKS[c][0]:
+                        for t in range(PACK):
+                            authorities(t, j0, n)
+            if c > 0:
+                add_residual(c - 1)
+            if inside:
+                round_z(c)
+            if c > 0:
+                round_result(c - 1)
+            if inside:
+                second_product(c)
+            if c > 0:
+                hand_out(c - 1)
         for q in range(4):
-            nc.scalar.dma_start(out=out_2[0, 4 * q : 4 * q + 4, :].bitcast(I32), in_=out_s[32 * q : 32 * q + 4, :].bitcast(I32))
+            (nc.scalar if q % 2 == 0 else nc.sync).dma_start(out=out_2[0, 4 * q : 4 * q + 4, :].bitcast(I32), in_=out_s[32 * q : 32 * q + 4, :].bitcast(I32))

@@ -19,7 +19,7 @@ S = 512
 H = 512
 HALF = 256
 CHUNKS = ((0, 128), (128, 128), (256, 128), (384, 128))
-GATHERS = ((0, 256), (256, 256))
+GATHERS = ()
 FLOPS = 2 * 2 * 512 * 512 * 512
 
 
@@ -48,63 +48,71 @@ def tile_picked_hubauth_none_po_kernel(
         def cols(tile, start, n):
             return tile[:, start // 16 : (start + n) // 16]
 
-        x_s = keep.tile([P, T], U8, name="x_s", tag="g0", align_bytes=64)
+        x_s = keep.tile([P, T], U8, name="x_s", align_bytes=64)
         w_s_raw = keep.tile([P, H], U8, name="w_s_raw", align_bytes=64)
-        nc.gpsimd.memset(x_s[:].bitcast(I32), 0)
-        nc.vector.memset(w_s_raw[:].bitcast(I32), 0)
+        nc.gpsimd.memset(w_s_raw[:].bitcast(I32), 0)
+        nc.vector.memset(x_s[:].bitcast(I32), 0)
+
+        seed = keep.tile([P, 1], F32, name="seed")
+        nc.vector.memset(seed[:], 0.0)
 
         offs_t = load_list(offs, "offs_t")
-        gain = keep.tile([P, PACK], F32, name="gain")
-        nc.scalar.dma_start(out=gain[:], in_=gn.rearrange("(p t) o -> p (t o)", t=PACK))
-        x_w = keep.tile([P, T], U32, name="x_w", tag="big", align_bytes=64)
-        nc.scalar.dma_start(out=x_w[:].bitcast(I32), in_=words_view(x_words))
         w1_raw = keep.tile([P, H], U32, name="w1_raw", tag="w_raw", align_bytes=64)
         nc.scalar.dma_start(out=w1_raw[:].bitcast(I32), in_=words_view(w1_words))
-        load_scale_rows([nc.sync] * 4, x_s, x_scales)
+        x_w = keep.tile([P, T], U32, name="x_w", tag="big", align_bytes=64)
+        nc.sync.dma_start(out=x_w[:].bitcast(I32), in_=words_view(x_words))
+        load_scale_rows([nc.scalar, nc.sync] * 2, x_s, x_scales)
         load_scale_rows([nc.gpsimd, nc.gpsimd, nc.sync, nc.sync], w_s_raw, w1_scales)
         o1_t = load_list(o1, "o1_t")
         o2_t = load_list(o2, "o2_t")
         i1_t = load_list(i1, "i1_t")
         i2_t = load_list(i2, "i2_t")
+        gain = keep.tile([P, PACK], F32, name="gain")
+        nc.sync.dma_start(out=gain[:], in_=gn.rearrange("(p t) o -> p (t o)", t=PACK))
 
-        def deal_words(dealt, raw):
-            nc.scalar.copy(
+        def deal_words(copy, dealt, raw):
+            copy(
                 out=dealt[:].rearrange("p (t c i) -> p c t i", t=PACK, i=4),
                 in_=raw[:].rearrange("p (c i t) -> p c t i", t=PACK, i=4),
             )
 
-        def deal_scales(dealt, raw):
-            nc.vector.tensor_copy(
+        def deal_scales(copy, dealt, raw):
+            copy(
                 out=dealt[:].rearrange("p (t m) -> p t m", t=PACK), in_=raw[:].rearrange("p (m t) -> p t m", t=PACK)
             )
 
         warm = keep.tile([P, 1], F32, name="warm")
-        nc.scalar.activation(warm[:], gain[:, 0:1], ACT.Abs_reciprocal_sqrt, bias=1.0)
+        nc.scalar.activation(warm[:], seed[:], ACT.Abs_reciprocal_sqrt, bias=1.0)
         w1_w = keep.tile([P, H], U32, name="w1_w", align_bytes=64)
         w1_s = keep.tile([P, H], U8, name="w1_s", align_bytes=64)
-        deal_words(w1_w, w1_raw)
+        deal_words(nc.scalar.copy, w1_w, w1_raw)
 
-        g_s = keep.tile([P, S], U8, name="g_s", align_bytes=64)
-        nc.vector.tensor_copy(g_s[:], x_s[:].indirect(offs_t[:]))
-        g_w = []
+        deal_scales(nc.gpsimd.tensor_copy, w1_s, w_s_raw)
+        g_w, g_s = [], []
         for h in range(2):
-            half = keep.tile([P, HALF], U32, name="g_w%d" % h, tag="g%d" % h, align_bytes=64)
-            nc.vector.tensor_copy(half[:], x_w[:].indirect(cols(offs_t, h * HALF, HALF)))
-            g_w.append(half)
-            if h == 0:
-                deal_scales(w1_s, w_s_raw)
+            g_s.append(keep.tile([P, HALF], U8, name="g_s%d" % h, align_bytes=64))
+            g_w.append(keep.tile([P, HALF], U32, name="g_w%d" % h, align_bytes=64))
+            nc.vector.tensor_copy(g_s[h][:], x_s[:].indirect(cols(offs_t, h * HALF, HALF)))
+            nc.vector.tensor_copy(g_w[h][:], x_w[:].indirect(cols(offs_t, h * HALF, HALF)))
 
-        y = [keep.tile([P, S], F32, name="y%d" % t) for t in range(PACK)]
+        y = [keep.tile([P, S if t == 0 else 2 * S], F32, name="y%d" % t) for t in range(PACK)]
+        last_first = keep.tile([P, S], F32, name="last_first")
+        first = [y[t + 1][:, S : 2 * S] for t in range(PACK - 1)] + [last_first[:]]
         y_ps = {}
-        for t in range(PACK):
-            for h in range(2):
-                acc = psum.tile([P, HALF], F32, name="y_ps", tag="bank%d" % (4 * h + t))
+        for t in range(2, PACK):
+            y_ps[t] = psum.tile([P, S], F32, name="y_ps", tag="bank%d" % t)
+        for h in range(2):
+            for t in range(PACK):
+                if t >= 2:
+                    acc = y_ps[t][:, h * HALF : (h + 1) * HALF]
+                else:
+                    acc = psum.tile([P, HALF], F32, name="y_ps", tag="bank%d" % (4 * h + t))[:]
                 nc.tensor.matmul_mx(
-                    out=acc[:],
+                    out=acc,
                     lhsT=w1_w[:, t * P : (t + 1) * P].bitcast(FP8X4),
                     lhsT_scale=w1_s[:, t * P : (t + 1) * P],
                     rhs=g_w[h][:].bitcast(FP8X4),
-                    rhs_scale=g_s[:, h * HALF : (h + 1) * HALF],
+                    rhs_scale=g_s[h][:],
                     start=True,
                     stop=True,
                 )
@@ -118,32 +126,35 @@ def tile_picked_hubauth_none_po_kernel(
         w2_w = keep.tile([P, H], U32, name="w2_w", align_bytes=64)
         w2_s = keep.tile([P, H], U8, name="w2_s", align_bytes=64)
 
-        hub = [keep.tile([P, S], F32, name="hub%d" % t) for t in range(PACK)]
-        hn = [keep.tile([P, S], F32, name="hn%d" % t) for t in range(PACK)]
+        hn = [keep.tile([P, 2 * S if t < PACK - 1 else S], F32, name="hn%d" % t) for t in range(PACK)]
+        last_hub = keep.tile([P, S], F32, name="last_hub")
+        hub = [hn[t][:, S : 2 * S] for t in range(PACK - 1)] + [last_hub[:]]
 
         def evacuate(t):
-            nc.scalar.copy(out=y[t][:, 0:HALF], in_=y_ps[0, t][:])
-            nc.vector.tensor_copy(out=y[t][:, HALF:S], in_=y_ps[1, t][:])
+            if t >= 2:
+                nc.vector.tensor_copy(out=y[t][:, 0:S], in_=y_ps[t][:])
+            else:
+                nc.scalar.copy(out=y[t][:, 0:HALF], in_=y_ps[0, t])
+                nc.vector.tensor_copy(out=y[t][:, HALF:S], in_=y_ps[1, t])
 
-        def hubs(t, h):
-            first = keep.tile([P, HALF], F32, name="first%d_%d" % (t, h))
-            nc.scalar.activation(first[:], y[t][:].indirect(cols(o1_t, h * HALF, HALF)), ACT.Copy)
+        def hubs(t, j0, n):
+            nc.scalar.activation(first[t][:, j0 : j0 + n], y[t][:].indirect(cols(o1_t, j0, n)), ACT.Copy)
             nc.vector.tensor_tensor(
-                hub[t][:, h * HALF : (h + 1) * HALF], y[t][:].indirect(cols(o2_t, h * HALF, HALF)), first[:], ALU.add
+                hub[t][:, j0 : j0 + n], y[t][:].indirect(cols(o2_t, j0, n)), first[t][:, j0 : j0 + n], ALU.add
             )
 
         square = [keep.tile([P, S], F32, name="square%d" % t) for t in range(PACK)]
 
         def squares(t):
             if "SSSV"[t] == "V":
-                nc.vector.tensor_tensor(square[t][:], hub[t][:], hub[t][:], ALU.mult)
+                nc.vector.tensor_tensor(square[t][:], hub[t], hub[t], ALU.mult)
             else:
-                nc.scalar.activation(square[t][:], hub[t][:], ACT.Square)
+                nc.scalar.activation(square[t][:], hub[t], ACT.Square)
 
         def normalise(t):
             root = keep.tile([P, S], F32, name="root%d" % t)
             nc.scalar.activation(root[:], square[t][:], ACT.Abs_reciprocal_sqrt, bias=1.0)
-            nc.vector.scalar_tensor_tensor(hn[t][:], hub[t][:], gain[:, t : t + 1], root[:], ALU.mult, ALU.mult)
+            nc.vector.scalar_tensor_tensor(hn[t][:, 0:S], hub[t], gain[:, t : t + 1], root[:], ALU.mult, ALU.mult)
 
         z = keep.tile([P, PACK, S], F32, name="z")
 
@@ -165,7 +176,7 @@ def tile_picked_hubauth_none_po_kernel(
         def round_z(c):
             j0, n = CHUNKS[c]
             z_b[c] = keep.tile([P, n, PACK], BF16, name="z_b%d" % c, align_bytes=64)
-            interleave("SSSV"[c], z_b[c], z[:, :, j0 : j0 + n])
+            interleave("SSSS"[c], z_b[c], z[:, :, j0 : j0 + n])
 
         def second_product(c):
             j0, n = CHUNKS[c]
@@ -216,24 +227,27 @@ def tile_picked_hubauth_none_po_kernel(
         for t in range(PACK):
             if 0 < t < PACK - 1:
                 evacuate(t + 1)
-            hubs(t, 0)
+            if t == 0:
+                hubs(t, 0, HALF)
+                hubs(t, HALF, HALF)
+            else:
+                hubs(t, 0, S)
             if t > 1:
                 normalise(t - 2)
-            hubs(t, 1)
             if t > 0:
                 squares(t - 1)
         normalise(PACK - 2)
         squares(PACK - 1)
         normalise(PACK - 1)
-        deal_scales(w2_s, w_s_raw)
-        deal_words(w2_w, w2_raw)
+        deal_scales(nc.vector.tensor_copy, w2_s, w_s_raw)
+        deal_words(nc.vector.tensor_copy, w2_w, w2_raw)
         for c in range(len(CHUNKS) + 1):
             inside = c < len(CHUNKS)
             if inside:
-                for j0, n in GATHERS:
-                    if j0 == CHUNKS[c][0]:
-                        for t in range(PACK):
-                            authorities(t, j0, n)
+                if c == 0:
+                    for t in range(PACK - 1):
+                        authorities(t, 0, S)
+                authorities(PACK - 1, *CHUNKS[c])
             if c > 0:
                 add_residual(c - 1)
             if inside:

@@ -17,9 +17,11 @@ PACK = 4
 T = 2048
 S = 512
 H = 512
-HALF = 256
-CHUNKS = ((0, 128), (128, 128), (256, 128), (384, 128))
-GATHERS = ()
+HALF = S // 2
+CHUNK = 128
+CHUNKS = S // CHUNK
+LAST = PACK - 1
+SHARED = 2
 FLOPS = 2 * 2 * 512 * 512 * 512
 
 
@@ -36,17 +38,39 @@ def tile_picked_hubauth_none_po_kernel(
         def words_view(dram):
             return dram[0].rearrange("p n t -> p (n t)").bitcast(I32)
 
-        def load_scale_rows(engines, plane, dram):
-            for q, engine in enumerate(engines):
-                engine.dma_start(out=plane[32 * q : 32 * q + 4, :].bitcast(I32), in_=dram[0, 4 * q : 4 * q + 4, :].bitcast(I32))
+        def load_scale_rows(queues, plane, dram):
+            for q, queue in enumerate(queues):
+                queue.dma_start(
+                    out=plane[32 * q : 32 * q + 4, :].bitcast(I32), in_=dram[0, 4 * q : 4 * q + 4, :].bitcast(I32)
+                )
 
         def load_list(dram, name):
-            tile = lists.tile([P, S // 16], U16, name=name)
-            nc.sync.dma_start(tile[:], dram)
-            return tile
+            offsets = lists.tile([P, S // 16], U16, name=name)
+            nc.sync.dma_start(offsets[:], dram)
+            return offsets
 
-        def cols(tile, start, n):
-            return tile[:, start // 16 : (start + n) // 16]
+        def entries(offsets, start, n):
+            return offsets[:, start // 16 : (start + n) // 16]
+
+        def deal_words(copy, dealt, raw):
+            copy(
+                out=dealt[:].rearrange("p (t c i) -> p c t i", t=PACK, i=4),
+                in_=raw[:].rearrange("p (c i t) -> p c t i", t=PACK, i=4),
+            )
+
+        def deal_scales(copy, dealt, raw):
+            copy(out=dealt[:].rearrange("p (t m) -> p t m", t=PACK), in_=raw[:].rearrange("p (m t) -> p t m", t=PACK))
+
+        def product(out, w_words, w_scales, t, words, scales):
+            nc.tensor.matmul_mx(
+                out=out,
+                lhsT=w_words[:, t * P : (t + 1) * P].bitcast(FP8X4),
+                lhsT_scale=w_scales[:, t * P : (t + 1) * P],
+                rhs=words[:].bitcast(FP8X4),
+                rhs_scale=scales[:],
+                start=True,
+                stop=True,
+            )
 
         x_s = keep.tile([P, T], U8, name="x_s", align_bytes=64)
         w_s_raw = keep.tile([P, H], U8, name="w_s_raw", align_bytes=64)
@@ -62,7 +86,7 @@ def tile_picked_hubauth_none_po_kernel(
         x_w = keep.tile([P, T], U32, name="x_w", tag="big", align_bytes=64)
         nc.sync.dma_start(out=x_w[:].bitcast(I32), in_=words_view(x_words))
         load_scale_rows([nc.scalar, nc.sync] * 2, x_s, x_scales)
-        load_scale_rows([nc.gpsimd, nc.gpsimd, nc.sync, nc.sync], w_s_raw, w1_scales)
+        load_scale_rows([nc.gpsimd, nc.sync, nc.sync, nc.sync], w_s_raw, w1_scales)
         o1_t = load_list(o1, "o1_t")
         o2_t = load_list(o2, "o2_t")
         i1_t = load_list(i1, "i1_t")
@@ -70,53 +94,37 @@ def tile_picked_hubauth_none_po_kernel(
         gain = keep.tile([P, PACK], F32, name="gain")
         nc.sync.dma_start(out=gain[:], in_=gn.rearrange("(p t) o -> p (t o)", t=PACK))
 
-        def deal_words(copy, dealt, raw):
-            copy(
-                out=dealt[:].rearrange("p (t c i) -> p c t i", t=PACK, i=4),
-                in_=raw[:].rearrange("p (c i t) -> p c t i", t=PACK, i=4),
-            )
-
-        def deal_scales(copy, dealt, raw):
-            copy(
-                out=dealt[:].rearrange("p (t m) -> p t m", t=PACK), in_=raw[:].rearrange("p (m t) -> p t m", t=PACK)
-            )
-
         warm = keep.tile([P, 1], F32, name="warm")
         nc.scalar.activation(warm[:], seed[:], ACT.Abs_reciprocal_sqrt, bias=1.0)
+
         w1_w = keep.tile([P, H], U32, name="w1_w", align_bytes=64)
         w1_s = keep.tile([P, H], U8, name="w1_s", align_bytes=64)
         deal_words(nc.scalar.copy, w1_w, w1_raw)
-
         deal_scales(nc.gpsimd.tensor_copy, w1_s, w_s_raw)
+
         g_w, g_s = [], []
         for h in range(2):
             g_s.append(keep.tile([P, HALF], U8, name="g_s%d" % h, align_bytes=64))
             g_w.append(keep.tile([P, HALF], U32, name="g_w%d" % h, align_bytes=64))
-            nc.vector.tensor_copy(g_s[h][:], x_s[:].indirect(cols(offs_t, h * HALF, HALF)))
-            nc.vector.tensor_copy(g_w[h][:], x_w[:].indirect(cols(offs_t, h * HALF, HALF)))
+            nc.vector.tensor_copy(g_s[h][:], x_s[:].indirect(entries(offs_t, h * HALF, HALF)))
+            nc.vector.tensor_copy(g_w[h][:], x_w[:].indirect(entries(offs_t, h * HALF, HALF)))
 
         y = [keep.tile([P, S if t == 0 else 2 * S], F32, name="y%d" % t) for t in range(PACK)]
         last_first = keep.tile([P, S], F32, name="last_first")
-        first = [y[t + 1][:, S : 2 * S] for t in range(PACK - 1)] + [last_first[:]]
-        y_ps = {}
-        for t in range(2, PACK):
-            y_ps[t] = psum.tile([P, S], F32, name="y_ps", tag="bank%d" % t)
-        for h in range(2):
-            for t in range(PACK):
-                if t >= 2:
-                    acc = y_ps[t][:, h * HALF : (h + 1) * HALF]
-                else:
-                    acc = psum.tile([P, HALF], F32, name="y_ps", tag="bank%d" % (4 * h + t))[:]
-                nc.tensor.matmul_mx(
-                    out=acc,
-                    lhsT=w1_w[:, t * P : (t + 1) * P].bitcast(FP8X4),
-                    lhsT_scale=w1_s[:, t * P : (t + 1) * P],
-                    rhs=g_w[h][:].bitcast(FP8X4),
-                    rhs_scale=g_s[h][:],
-                    start=True,
-                    stop=True,
-                )
-                y_ps[h, t] = acc
+        first = [y[t + 1][:, S : 2 * S] for t in range(LAST)] + [last_first[:]]
+
+        y_whole, y_half = {}, {}
+        for t in range(SHARED, PACK):
+            y_whole[t] = psum.tile([P, S], F32, name="y_ps", tag="bank%d" % t)
+        for pair in range(2):
+            for h in range(2):
+                for t in (2 * pair, 2 * pair + 1):
+                    if t >= SHARED:
+                        acc = y_whole[t][:, h * HALF : (h + 1) * HALF]
+                    else:
+                        acc = psum.tile([P, HALF], F32, name="y_ps", tag="bank%d" % (PACK * h + t))[:]
+                        y_half[h, t] = acc
+                    product(acc, w1_w, w1_s, t, g_w[h], g_s[h])
 
         w2_raw = keep.tile([P, H], U32, name="w2_raw", tag="w_raw", align_bytes=64)
         nc.sync.dma_start(out=w2_raw[:].bitcast(I32), in_=words_view(w2_words))
@@ -126,27 +134,27 @@ def tile_picked_hubauth_none_po_kernel(
         w2_w = keep.tile([P, H], U32, name="w2_w", align_bytes=64)
         w2_s = keep.tile([P, H], U8, name="w2_s", align_bytes=64)
 
-        hn = [keep.tile([P, 2 * S if t < PACK - 1 else S], F32, name="hn%d" % t) for t in range(PACK)]
+        hn = [keep.tile([P, 2 * S if t < LAST else S], F32, name="hn%d" % t) for t in range(PACK)]
         last_hub = keep.tile([P, S], F32, name="last_hub")
-        hub = [hn[t][:, S : 2 * S] for t in range(PACK - 1)] + [last_hub[:]]
+        hub = [hn[t][:, S : 2 * S] for t in range(LAST)] + [last_hub[:]]
 
         def evacuate(t):
-            if t >= 2:
-                nc.vector.tensor_copy(out=y[t][:, 0:S], in_=y_ps[t][:])
+            if t >= SHARED:
+                nc.vector.tensor_copy(out=y[t][:, 0:S], in_=y_whole[t][:])
             else:
-                nc.scalar.copy(out=y[t][:, 0:HALF], in_=y_ps[0, t])
-                nc.vector.tensor_copy(out=y[t][:, HALF:S], in_=y_ps[1, t])
+                nc.scalar.copy(out=y[t][:, 0:HALF], in_=y_half[0, t])
+                nc.vector.tensor_copy(out=y[t][:, HALF:S], in_=y_half[1, t])
 
         def hubs(t, j0, n):
-            nc.scalar.activation(first[t][:, j0 : j0 + n], y[t][:].indirect(cols(o1_t, j0, n)), ACT.Copy)
+            nc.scalar.activation(first[t][:, j0 : j0 + n], y[t][:].indirect(entries(o1_t, j0, n)), ACT.Copy)
             nc.vector.tensor_tensor(
-                hub[t][:, j0 : j0 + n], y[t][:].indirect(cols(o2_t, j0, n)), first[t][:, j0 : j0 + n], ALU.add
+                hub[t][:, j0 : j0 + n], y[t][:].indirect(entries(o2_t, j0, n)), first[t][:, j0 : j0 + n], ALU.add
             )
 
         square = [keep.tile([P, S], F32, name="square%d" % t) for t in range(PACK)]
 
         def squares(t):
-            if "SSSV"[t] == "V":
+            if t == LAST:
                 nc.vector.tensor_tensor(square[t][:], hub[t], hub[t], ALU.mult)
             else:
                 nc.scalar.activation(square[t][:], hub[t], ACT.Square)
@@ -160,72 +168,57 @@ def tile_picked_hubauth_none_po_kernel(
 
         def authorities(t, j0, n):
             one = keep.tile([P, n], F32, name="one%d_%d" % (t, j0))
-            nc.scalar.activation(one[:], hn[t][:].indirect(cols(i1_t, j0, n)), ACT.Copy)
-            nc.vector.tensor_tensor(z[:, t, j0 : j0 + n], hn[t][:].indirect(cols(i2_t, j0, n)), one[:], ALU.add)
+            nc.scalar.activation(one[:], hn[t][:].indirect(entries(i1_t, j0, n)), ACT.Copy)
+            nc.vector.tensor_tensor(z[:, t, j0 : j0 + n], hn[t][:].indirect(entries(i2_t, j0, n)), one[:], ALU.add)
 
-        def interleave(engine, grouped, planes):
-            copy = nc.vector.tensor_copy if engine == "V" else nc.scalar.copy
-            copy(out=grouped[:], in_=planes.rearrange("p t j -> p j t"))
+        def round_and_group(copy, grouped, slabs):
+            copy(out=grouped[:], in_=slabs.rearrange("p t j -> p j t"))
 
         out_s = keep.tile([P, S], U8, name="out_s", align_bytes=64)
+        out_w = keep.tile([P, S], U32, name="out_w", align_bytes=64)
         out_rows = out_0.rearrange("(p t) j -> p t j", t=PACK)
         out_words = words_view(out_1)
 
-        z_b, banks, result, r_b = {}, {}, {}, {}
+        z_b, o_ps, result, r_b = {}, {}, {}, {}
+
+        def columns(c):
+            return slice(c * CHUNK, (c + 1) * CHUNK)
 
         def round_z(c):
-            j0, n = CHUNKS[c]
-            z_b[c] = keep.tile([P, n, PACK], BF16, name="z_b%d" % c, align_bytes=64)
-            interleave("SSSS"[c], z_b[c], z[:, :, j0 : j0 + n])
+            z_b[c] = keep.tile([P, CHUNK, PACK], BF16, name="z_b%d" % c, align_bytes=64)
+            round_and_group(nc.scalar.copy, z_b[c], z[:, :, columns(c)])
 
         def second_product(c):
-            j0, n = CHUNKS[c]
-            z_w = keep.tile([P, n], U32, name="z_w%d" % c, align_bytes=64)
-            z_s = keep.tile([P, n], U8, name="z_s%d" % c, align_bytes=64)
+            z_w = keep.tile([P, CHUNK], U32, name="z_w%d" % c, align_bytes=64)
+            z_s = keep.tile([P, CHUNK], U8, name="z_s%d" % c, align_bytes=64)
             nc.vector.quantize_mx(out=z_w[:].bitcast(FP8X4), scales=z_s[:], in_=z_b[c][:].rearrange("p j t -> p (j t)"))
-            per_bank = S // n
-            banks[c] = []
-            for b in range(PACK // per_bank):
-                acc = psum.tile([P, per_bank, n], F32, name="o_ps", tag="bank%d" % (j0 // P + b))
-                for u in range(per_bank):
-                    t = b * per_bank + u
-                    nc.tensor.matmul_mx(
-                        out=acc[:, u, :],
-                        lhsT=w2_w[:, t * P : (t + 1) * P].bitcast(FP8X4),
-                        lhsT_scale=w2_s[:, t * P : (t + 1) * P],
-                        rhs=z_w[:].bitcast(FP8X4),
-                        rhs_scale=z_s[:],
-                        start=True,
-                        stop=True,
-                    )
-                banks[c].append(acc)
+            o_ps[c] = psum.tile([P, PACK, CHUNK], F32, name="o_ps", tag="bank%d" % c)
+            for t in range(PACK):
+                product(o_ps[c][:, t, :], w2_w, w2_s, t, z_w, z_s)
 
         def add_residual(c):
-            j0, n = CHUNKS[c]
-            per_bank = S // n
-            result[c] = keep.tile([P, PACK, n], F32, name="result%d" % c)
-            for b, acc in enumerate(banks[c]):
-                rows = slice(b * per_bank, (b + 1) * per_bank)
-                nc.vector.tensor_tensor(result[c][:, rows, :], acc[:], res_t[:, rows, j0 : j0 + n], ALU.add)
-            nc.sync.dma_start(out=out_rows[:, :, j0 : j0 + n], in_=result[c][:])
+            result[c] = keep.tile([P, PACK, CHUNK], F32, name="result%d" % c)
+            nc.vector.tensor_tensor(result[c][:], o_ps[c][:], res_t[:, :, columns(c)], ALU.add)
+            nc.sync.dma_start(out=out_rows[:, :, columns(c)], in_=result[c][:])
 
         def round_result(c):
-            j0, n = CHUNKS[c]
-            r_b[c] = keep.tile([P, n, PACK], BF16, name="r_b%d" % c, align_bytes=64)
-            interleave("SSSV"[c], r_b[c], result[c][:])
+            r_b[c] = keep.tile([P, CHUNK, PACK], BF16, name="r_b%d" % c, align_bytes=64)
+            round_and_group(nc.vector.tensor_copy if c == CHUNKS - 1 else nc.scalar.copy, r_b[c], result[c][:])
 
         def hand_out(c):
-            j0, n = CHUNKS[c]
-            r_w = keep.tile([P, n], U32, name="r_w%d" % c, align_bytes=64)
             nc.vector.quantize_mx(
-                out=r_w[:].bitcast(FP8X4), scales=out_s[:, j0 : j0 + n], in_=r_b[c][:].rearrange("p j t -> p (j t)")
+                out=out_w[:, columns(c)].bitcast(FP8X4),
+                scales=out_s[:, columns(c)],
+                in_=r_b[c][:].rearrange("p j t -> p (j t)"),
             )
-            nc.sync.dma_start(out=out_words[:, j0 : j0 + n], in_=r_w[:].bitcast(I32))
+            if c >= CHUNKS - 2:
+                span = columns(c) if c == CHUNKS - 1 else slice(0, (c + 1) * CHUNK)
+                nc.sync.dma_start(out=out_words[:, span], in_=out_w[:, span].bitcast(I32))
 
         evacuate(0)
         evacuate(1)
         for t in range(PACK):
-            if 0 < t < PACK - 1:
+            if 0 < t < LAST:
                 evacuate(t + 1)
             if t == 0:
                 hubs(t, 0, HALF)
@@ -236,27 +229,29 @@ def tile_picked_hubauth_none_po_kernel(
                 normalise(t - 2)
             if t > 0:
                 squares(t - 1)
-        normalise(PACK - 2)
-        squares(PACK - 1)
-        normalise(PACK - 1)
+        normalise(LAST - 1)
+        squares(LAST)
+        normalise(LAST)
         deal_scales(nc.vector.tensor_copy, w2_s, w_s_raw)
         deal_words(nc.vector.tensor_copy, w2_w, w2_raw)
-        for c in range(len(CHUNKS) + 1):
-            inside = c < len(CHUNKS)
-            if inside:
-                if c == 0:
-                    for t in range(PACK - 1):
-                        authorities(t, 0, S)
-                authorities(PACK - 1, *CHUNKS[c])
+        for t in range(LAST):
+            authorities(t, 0, S)
+
+        for c in range(CHUNKS + 1):
+            if c < CHUNKS:
+                authorities(LAST, c * CHUNK, CHUNK)
             if c > 0:
                 add_residual(c - 1)
-            if inside:
+            if c < CHUNKS:
                 round_z(c)
             if c > 0:
                 round_result(c - 1)
-            if inside:
+            if c < CHUNKS:
                 second_product(c)
             if c > 0:
                 hand_out(c - 1)
-        for q in range(4):
-            (nc.scalar if q % 2 == 0 else nc.sync).dma_start(out=out_2[0, 4 * q : 4 * q + 4, :].bitcast(I32), in_=out_s[32 * q : 32 * q + 4, :].bitcast(I32))
+
+        for q, queue in enumerate([nc.scalar, nc.sync] * 2):
+            queue.dma_start(
+                out=out_2[0, 4 * q : 4 * q + 4, :].bitcast(I32), in_=out_s[32 * q : 32 * q + 4, :].bitcast(I32)
+            )

from contextlib import ExitStack

import concourse.mybir as mybir

F32 = mybir.dt.float32
BF16 = mybir.dt.bfloat16
I32 = mybir.dt.int32
U32 = mybir.dt.uint32
U16 = mybir.dt.uint16
U8 = mybir.dt.uint8
FP8X4 = mybir.dt.float8_e4m3fn_x4
ACT = mybir.ActivationFunctionType
ALU = mybir.AluOpType

P = 128
PACK = 4
T = 2048
S = 512
H = 512
HALF = S // 2
CHUNK = 128
CHUNKS = S // CHUNK
LAST = PACK - 1
SHARED = 2
FLOPS = 2 * 2 * 512 * 512 * 512


def tile_picked_hubauth_none_po_kernel(
    tc, x_words, x_scales, w1_words, w1_scales, gn, w2_words, w2_scales, res, offs, o1, o2, i1, i2,
    out_0, out_1, out_2,
):
    nc = tc.nc
    with ExitStack() as ctx:
        lists = ctx.enter_context(tc.tile_pool(name="lists", bufs=1))
        keep = ctx.enter_context(tc.tile_pool(name="keep", bufs=1))
        psum = ctx.enter_context(tc.psum_pool(name="psum", bufs=1))

        def words_view(dram):
            return dram[0].rearrange("p n t -> p (n t)").bitcast(I32)

        def load_scale_rows(queues, plane, dram):
            for q, queue in enumerate(queues):
                queue.dma_start(
                    out=plane[32 * q : 32 * q + 4, :].bitcast(I32), in_=dram[0, 4 * q : 4 * q + 4, :].bitcast(I32)
                )

        def load_list(dram, name):
            offsets = lists.tile([P, S // 16], U16, name=name)
            nc.sync.dma_start(offsets[:], dram)
            return offsets

        def entries(offsets, start, n):
            return offsets[:, start // 16 : (start + n) // 16]

        def deal_words(copy, dealt, raw):
            copy(
                out=dealt[:].rearrange("p (t c i) -> p c t i", t=PACK, i=4),
                in_=raw[:].rearrange("p (c i t) -> p c t i", t=PACK, i=4),
            )

        def deal_scales(copy, dealt, raw):
            copy(out=dealt[:].rearrange("p (t m) -> p t m", t=PACK), in_=raw[:].rearrange("p (m t) -> p t m", t=PACK))

        def product(out, w_words, w_scales, t, words, scales):
            nc.tensor.matmul_mx(
                out=out,
                lhsT=w_words[:, t * P : (t + 1) * P].bitcast(FP8X4),
                lhsT_scale=w_scales[:, t * P : (t + 1) * P],
                rhs=words[:].bitcast(FP8X4),
                rhs_scale=scales[:],
                start=True,
                stop=True,
            )

        x_s = keep.tile([P, T], U8, name="x_s", align_bytes=64)
        w_s_raw = keep.tile([P, H], U8, name="w_s_raw", align_bytes=64)
        nc.gpsimd.memset(w_s_raw[:].bitcast(I32), 0)
        nc.vector.memset(x_s[:].bitcast(I32), 0)

        seed = keep.tile([P, 1], F32, name="seed")
        nc.vector.memset(seed[:], 0.0)

        offs_t = load_list(offs, "offs_t")
        w1_raw = keep.tile([P, H], U32, name="w1_raw", tag="w_raw", align_bytes=64)
        nc.scalar.dma_start(out=w1_raw[:].bitcast(I32), in_=words_view(w1_words))
        x_w = keep.tile([P, T], U32, name="x_w", tag="big", align_bytes=64)
        nc.sync.dma_start(out=x_w[:].bitcast(I32), in_=words_view(x_words))
        load_scale_rows([nc.scalar, nc.sync] * 2, x_s, x_scales)
        load_scale_rows([nc.gpsimd, nc.sync, nc.sync, nc.sync], w_s_raw, w1_scales)
        o1_t = load_list(o1, "o1_t")
        o2_t = load_list(o2, "o2_t")
        i1_t = load_list(i1, "i1_t")
        i2_t = load_list(i2, "i2_t")
        gain = keep.tile([P, PACK], F32, name="gain")
        nc.sync.dma_start(out=gain[:], in_=gn.rearrange("(p t) o -> p (t o)", t=PACK))

        warm = keep.tile([P, 1], F32, name="warm")
        nc.scalar.activation(warm[:], seed[:], ACT.Abs_reciprocal_sqrt, bias=1.0)

        w1_w = keep.tile([P, H], U32, name="w1_w", align_bytes=64)
        w1_s = keep.tile([P, H], U8, name="w1_s", align_bytes=64)
        deal_words(nc.scalar.copy, w1_w, w1_raw)
        deal_scales(nc.gpsimd.tensor_copy, w1_s, w_s_raw)

        g_w, g_s = [], []
        for h in range(2):
            g_s.append(keep.tile([P, HALF], U8, name="g_s%d" % h, align_bytes=64))
            g_w.append(keep.tile([P, HALF], U32, name="g_w%d" % h, align_bytes=64))
            nc.vector.tensor_copy(g_s[h][:], x_s[:].indirect(entries(offs_t, h * HALF, HALF)))
            nc.vector.tensor_copy(g_w[h][:], x_w[:].indirect(entries(offs_t, h * HALF, HALF)))

        y = [keep.tile([P, S if t == 0 else 2 * S], F32, name="y%d" % t) for t in range(PACK)]
        last_first = keep.tile([P, S], F32, name="last_first")
        first = [y[t + 1][:, S : 2 * S] for t in range(LAST)] + [last_first[:]]

        y_whole, y_half = {}, {}
        for t in range(SHARED, PACK):
            y_whole[t] = psum.tile([P, S], F32, name="y_ps", tag="bank%d" % t)
        for pair in range(2):
            for h in range(2):
                for t in (2 * pair, 2 * pair + 1):
                    if t >= SHARED:
                        acc = y_whole[t][:, h * HALF : (h + 1) * HALF]
                    else:
                        acc = psum.tile([P, HALF], F32, name="y_ps", tag="bank%d" % (PACK * h + t))[:]
                        y_half[h, t] = acc
                    product(acc, w1_w, w1_s, t, g_w[h], g_s[h])

        w2_raw = keep.tile([P, H], U32, name="w2_raw", tag="w_raw", align_bytes=64)
        nc.sync.dma_start(out=w2_raw[:].bitcast(I32), in_=words_view(w2_words))
        load_scale_rows([nc.sync] * 4, w_s_raw, w2_scales)
        res_t = keep.tile([P, PACK, S], F32, name="res_t", tag="big", align_bytes=64)
        nc.sync.dma_start(out=res_t[:], in_=res.rearrange("(p t) j -> p t j", t=PACK))
        w2_w = keep.tile([P, H], U32, name="w2_w", align_bytes=64)
        w2_s = keep.tile([P, H], U8, name="w2_s", align_bytes=64)

        hn = [keep.tile([P, 2 * S if t < LAST else S], F32, name="hn%d" % t) for t in range(PACK)]
        last_hub = keep.tile([P, S], F32, name="last_hub")
        hub = [hn[t][:, S : 2 * S] for t in range(LAST)] + [last_hub[:]]

        def evacuate(t):
            if t >= SHARED:
                nc.vector.tensor_copy(out=y[t][:, 0:S], in_=y_whole[t][:])
            else:
                nc.scalar.copy(out=y[t][:, 0:HALF], in_=y_half[0, t])
                nc.vector.tensor_copy(out=y[t][:, HALF:S], in_=y_half[1, t])

        def hubs(t, j0, n):
            nc.scalar.activation(first[t][:, j0 : j0 + n], y[t][:].indirect(entries(o1_t, j0, n)), ACT.Copy)
            nc.vector.tensor_tensor(
                hub[t][:, j0 : j0 + n], y[t][:].indirect(entries(o2_t, j0, n)), first[t][:, j0 : j0 + n], ALU.add
            )

        square = [keep.tile([P, S], F32, name="square%d" % t) for t in range(PACK)]

        def squares(t):
            if t == LAST:
                nc.vector.tensor_tensor(square[t][:], hub[t], hub[t], ALU.mult)
            else:
                nc.scalar.activation(square[t][:], hub[t], ACT.Square)

        def normalise(t):
            root = keep.tile([P, S], F32, name="root%d" % t)
            nc.scalar.activation(root[:], square[t][:], ACT.Abs_reciprocal_sqrt, bias=1.0)
            nc.vector.scalar_tensor_tensor(hn[t][:, 0:S], hub[t], gain[:, t : t + 1], root[:], ALU.mult, ALU.mult)

        z = keep.tile([P, PACK, S], F32, name="z")

        def authorities(t, j0, n):
            one = keep.tile([P, n], F32, name="one%d_%d" % (t, j0))
            nc.scalar.activation(one[:], hn[t][:].indirect(entries(i1_t, j0, n)), ACT.Copy)
            nc.vector.tensor_tensor(z[:, t, j0 : j0 + n], hn[t][:].indirect(entries(i2_t, j0, n)), one[:], ALU.add)

        def round_and_group(copy, grouped, slabs):
            copy(out=grouped[:], in_=slabs.rearrange("p t j -> p j t"))

        out_s = keep.tile([P, S], U8, name="out_s", align_bytes=64)
        out_w = keep.tile([P, S], U32, name="out_w", align_bytes=64)
        out_rows = out_0.rearrange("(p t) j -> p t j", t=PACK)
        out_words = words_view(out_1)

        z_b, o_ps, result, r_b = {}, {}, {}, {}

        def columns(c):
            return slice(c * CHUNK, (c + 1) * CHUNK)

        def round_z(c):
            z_b[c] = keep.tile([P, CHUNK, PACK], BF16, name="z_b%d" % c, align_bytes=64)
            round_and_group(nc.scalar.copy, z_b[c], z[:, :, columns(c)])

        def second_product(c):
            z_w = keep.tile([P, CHUNK], U32, name="z_w%d" % c, align_bytes=64)
            z_s = keep.tile([P, CHUNK], U8, name="z_s%d" % c, align_bytes=64)
            nc.vector.quantize_mx(out=z_w[:].bitcast(FP8X4), scales=z_s[:], in_=z_b[c][:].rearrange("p j t -> p (j t)"))
            o_ps[c] = psum.tile([P, PACK, CHUNK], F32, name="o_ps", tag="bank%d" % c)
            for t in range(PACK):
                product(o_ps[c][:, t, :], w2_w, w2_s, t, z_w, z_s)

        def add_residual(c):
            result[c] = keep.tile([P, PACK, CHUNK], F32, name="result%d" % c)
            nc.vector.tensor_tensor(result[c][:], o_ps[c][:], res_t[:, :, columns(c)], ALU.add)
            nc.sync.dma_start(out=out_rows[:, :, columns(c)], in_=result[c][:])

        def round_result(c):
            r_b[c] = keep.tile([P, CHUNK, PACK], BF16, name="r_b%d" % c, align_bytes=64)
            round_and_group(nc.vector.tensor_copy if c == CHUNKS - 1 else nc.scalar.copy, r_b[c], result[c][:])

        def hand_out(c):
            nc.vector.quantize_mx(
                out=out_w[:, columns(c)].bitcast(FP8X4),
                scales=out_s[:, columns(c)],
                in_=r_b[c][:].rearrange("p j t -> p (j t)"),
            )
            if c >= CHUNKS - 2:
                span = columns(c) if c == CHUNKS - 1 else slice(0, (c + 1) * CHUNK)
                nc.sync.dma_start(out=out_words[:, span], in_=out_w[:, span].bitcast(I32))

        evacuate(0)
        evacuate(1)
        for t in range(PACK):
            if 0 < t < LAST:
                evacuate(t + 1)
            if t == 0:
                hubs(t, 0, HALF)
                hubs(t, HALF, HALF)
            else:
                hubs(t, 0, S)
            if t > 1:
                normalise(t - 2)
            if t > 0:
                squares(t - 1)
        normalise(LAST - 1)
        squares(LAST)
        normalise(LAST)
        deal_scales(nc.vector.tensor_copy, w2_s, w_s_raw)
        deal_words(nc.vector.tensor_copy, w2_w, w2_raw)
        for t in range(LAST):
            authorities(t, 0, S)

        for c in range(CHUNKS + 1):
            if c < CHUNKS:
                authorities(LAST, c * CHUNK, CHUNK)
            if c > 0:
                add_residual(c - 1)
            if c < CHUNKS:
                round_z(c)
            if c > 0:
                round_result(c - 1)
            if c < CHUNKS:
                second_product(c)
            if c > 0:
                hand_out(c - 1)

        for q, queue in enumerate([nc.scalar, nc.sync] * 2):
            queue.dma_start(
                out=out_2[0, 4 * q : 4 * q + 4, :].bitcast(I32), in_=out_s[32 * q : 32 * q + 4, :].bitcast(I32)
            )
